import numpy as np, ml_dtypes
CORES = [1,17,65,89,97,113]
N = 6
KB, QP = 1, 256
MEM = [0,2,5]
def setup_inputs(rng):
    q = rng.standard_normal((N, 128, QP), dtype=np.float32) / 4; k = rng.standard_normal((N, 128, KB * 128), dtype=np.float32)
    a = 2 * np.pi * rng.random((N, QP)); s = 400 * rng.random((N, QP)) ** 1.5; q[:, 0, :] = s * np.cos(a); q[:, 1, :] = s * np.sin(a); q[:, 2, :] = 150 * rng.standard_normal((N, QP)); k[:, 2, :] = 1 + k[:, 2, :] / 50
    c = np.zeros(N); c[MEM] = rng.permutation(len(MEM))
    a = (2 * np.pi * rng.random() + np.pi / 2 * (c.reshape(N, 1, 1) + 0.5) / len(MEM) - 0.5 + (np.arange(KB).reshape(1, KB, 1) + rng.random((N, KB, 128))) / KB).reshape(N, KB * 128); k[:, 0, :] = np.cos(a); k[:, 1, :] = np.sin(a)
    return {"q": q.astype(ml_dtypes.bfloat16), "k": k.astype(ml_dtypes.bfloat16), "v": rng.standard_normal((N, 128, KB * 128), dtype=np.float32).astype(ml_dtypes.bfloat16)}
def setup_inputs_big(rng):
    d = setup_inputs(rng)
    for k in ("v",): d[k] = (d[k].astype(np.float32) * 1048576.0).astype(d[k].dtype)
    return d
def setup_inputs_small(rng):
    d = setup_inputs(rng)
    for k in ("v",): d[k] = (d[k].astype(np.float32) * (1 / 1048576.0)).astype(d[k].dtype)
    return d
def reference(q, k, v):
    Q, K, V = q.astype(np.float64), k.astype(np.float64), v.astype(np.float64)
    y = np.zeros((N, QP, 128))
    for r in range(N):
        js = list(MEM)
        S = np.concatenate([K[j].T @ Q[r] for j in js], axis=0)
        P = np.exp(S - S.max(axis=0)); P = P / P.sum(axis=0)
        y[r] = P.T @ np.concatenate([V[j][:, 128 * b:128 * b + 128] for j in js for b in range(KB)], axis=0)
    return {"y": y.astype(ml_dtypes.bfloat16)}

@@ -1,0 +1,193 @@
+from concourse.bass import DstId, RemoteDMATransfer
+from concourse.mybir import AluOpType, AxisListType, ActivationFunctionType
+
+NS = 3
+SW = 264
+N_ON = 4
+N_RELAY = 8
+N_DIR = 8
+
+SCRATCH = {
+    "qs": ("sbuf", [128, 256], "bfloat16"),
+    "kv": ("sbuf", [128, NS * SW], "bfloat16"),
+    "kd": ("dram", [128, 128], "bfloat16"),
+    "vd": ("dram", [128, 128], "bfloat16"),
+    "one": ("sbuf", [128, 128], "bfloat16"),
+    "idn": ("sbuf", [128, 128], "bfloat16"),
+    "dg": ("sbuf", [128, 256], "bfloat16"),
+    "ngm": ("sbuf", [128, 2], "float32"),
+    "rl": ("sbuf", [128, 2], "float32"),
+    "pp": ("sbuf", [128, NS * 256], "bfloat16"),
+    "ys": ("sbuf", [128, 256], "bfloat16"),
+    "st0": ("psum", [128, 512], "float32"),
+    "st1": ("psum", [128, 512], "float32"),
+    "sc0": ("psum", [128, 512], "float32"),
+    "sc1": ("psum", [128, 512], "float32"),
+    "sc2": ("psum", [128, 512], "float32"),
+    "o0": ("psum", [128, 512], "float32"),
+    "o1": ("psum", [128, 512], "float32"),
+}
+SEMAPHORES = (["s_kd", "s_vd", "s_q", "s_c", "s_id", "s_pad", "s_st0", "s_st1", "s_m0", "s_m1", "s_dg",
+               "s_O0", "s_O1", "s_r0", "s_r1", "s_y0", "s_y1", "s_o0", "s_o1", "hK", "hV", "sent"]
+              + ["arrK%d" % i for i in range(NS)] + ["arrV%d" % i for i in range(NS)]
+              + ["s_S%d" % i for i in range(NS)] + ["s_P%d" % i for i in range(NS)])
+
+
+def bits(m):
+    return [e for e in range(m.bit_length()) if (m >> e) & 1]
+
+
+def pick(es, n):
+    return es[::len(es) // n][:n]
+
+
+def xfer(topo, src_ap, dst_ap, dsts, engines, sem):
+    ids = []
+    for d in dsts:
+        a = topo.addr(d)
+        ids.append(DstId(rid=a[0], pnc=a[1]))
+    return RemoteDMATransfer(dst_ids=ids, dma_engine_mask=sum(1 << e for e in engines), remote_sem=sem,
+                             srcs=[src_ap], dsts=[dst_ap] * len(dsts), alu_op=0)
+
+
+def plan(T, topo):
+    cores = list(T.cores)
+    out = []
+    for slot, j in enumerate(T.tables["MEM"]):
+        s = cores[j]
+        dests = [d for d in cores if d != s]
+        direct = [d for d in dests if topo.may_write(s, d)]
+        far = [d for d in dests if not topo.may_write(s, d)]
+        free = [c for c in range(topo.CHIPS * topo.CORES_PER_CHIP)
+                if topo.chip(c) == topo.chip(s) and c not in cores]
+        able = [c for c in free if all(topo.may_write(c, d) for d in far)]
+        out.append({"slot": slot, "src": s, "direct": direct, "far": far,
+                    "kh": [c for c in able if topo.die(c) == topo.die(s)][0],
+                    "vh": [c for c in able if topo.die(c) != topo.die(s)][0]})
+    return out
+
+
+def rank_program(g, core, T, topo):
+    sem = T.sem
+    P = plan(T, topo)
+
+    for p in P:
+        c0 = p["slot"] * SW
+        for who, hs, buf, off, arr in (("kh", sem.hK, T.kd, 0, "arrK%d"), ("vh", sem.hV, T.vd, 128, "arrV%d")):
+            if p["far"] and core == p[who]:
+                e = pick(bits(topo.mask(core, p["far"][0])), N_RELAY)
+                g.wait_ge(hs, N_ON)
+                g.remote_dma_fused([xfer(topo, buf[:], T.kv[:, c0 + off:c0 + off + 128], p["far"], e,
+                                         sem[arr % p["slot"]])], local_sem=sem.sent)
+                g.wait_ge(sem.sent, len(e))
+                return
+    if T.rank_of(core) is None:
+        return
+
+    mine = [p for p in P if p["src"] == core]
+    pe, dve, act, sy = g.tensor, g.vector, g.scalar, g.sync
+    mult, Exp, Copy = AluOpType.mult, ActivationFunctionType.Exp, ActivationFunctionType.Copy
+
+    if mine:
+        c0 = mine[0]["slot"] * SW
+        own = mine[0]["slot"]
+        sy.dma_start(T.kd[:], T.k[:]).then_inc(sem.s_kd, 16)
+        act.dma_start(T.vd[:], T.v[:]).then_inc(sem.s_vd, 16)
+        sy.dma_start(T.kv[:, c0:c0 + 128], T.k[:]).then_inc(sem["arrK%d" % own], 16)
+        act.dma_start(T.kv[:, c0 + 128:c0 + 256], T.v[:]).then_inc(sem["arrV%d" % own], 16)
+    sy.dma_start(T.qs[:], T.q[:]).then_inc(sem.s_q, 16)
+
+    dve.memset(T.one[:], 1.0).then_inc(sem.s_c, 1)
+    g.wait_ge(sem.s_c, 1)
+    g.affine_select(T.idn[:], T.one[:], [[-1, 128]], AluOpType.is_equal, 0.0, 0, 1).then_inc(sem.s_id, 1)
+    act.wait_ge(sem.s_c, 1)
+    act.activation(T.kv[:, 256::SW], T.one[:, 0:NS], Exp, scale=0.0).then_inc(sem.s_pad, 1)
+
+    if mine:
+        p = mine[0]
+        sent = 0
+        eng = bits(topo.mask(core, p["direct"][0]))
+        if p["far"]:
+            ek, ev = eng[0::2][:N_ON], eng[1::2][:N_ON]
+            g.wait_ge(sem.s_kd, 16)
+            g.wait_ge(sem.s_vd, 16)
+            g.remote_dma_fused([xfer(topo, T.kd[:], T.kd[:], [p["kh"]], ek, sem.hK),
+                                xfer(topo, T.vd[:], T.vd[:], [p["vh"]], ev, sem.hV)], local_sem=sem.sent)
+            sent += len(ek) + len(ev)
+        ed = pick(eng, N_DIR)
+        g.wait_ge(sem["arrK%d" % own], 16)
+        g.wait_ge(sem["arrV%d" % own], 16)
+        g.remote_dma_fused([xfer(topo, T.kv[:, c0:c0 + 256], T.kv[:, c0:c0 + 256], p["direct"], ed,
+                                 sem["arrK%d" % own])], local_sem=sem.sent)
+        sent += len(ed)
+        g.wait_ge(sem.sent, sent)
+
+    order = sorted(P, key=lambda p: (p["src"] != core, p["slot"]))
+    kw, vw = {}, {}
+    for p in P:
+        i = p["slot"]
+        if p["src"] == core:
+            kw[i], vw[i] = 16, 16
+        elif core in p["direct"]:
+            kw[i], vw[i] = N_DIR, 0
+        else:
+            kw[i], vw[i] = N_RELAY, N_RELAY
+    st = [T.st0, T.st1]
+    sc = [T.sc0, T.sc1, T.sc2]
+    ob = [T.o0, T.o1]
+
+    pe.wait_ge(sem.s_q, 16)
+    for p in order:
+        i = p["slot"]
+        K = T.kv[:, i * SW:i * SW + 128]
+        pe.wait_ge(sem["arrK%d" % i], kw[i])
+        pe.matmul(st[0][:, i * 128:(i + 1) * 128], T.qs[:, 0:128], K, True, True).then_inc(sem.s_st0, 1)
+        pe.matmul(st[1][:, i * 128:(i + 1) * 128], T.qs[:, 128:256], K, True, True).then_inc(sem.s_st1, 1)
+        pe.matmul(sc[i][:, 0:256], K, T.qs[:], True, False).then_inc(sem["s_S%d" % i], 1)
+
+    dve.wait_ge(sem.s_st0, NS)
+    dve.tensor_reduce(T.ngm[:, 0:1], st[0][:, 0:NS * 128], AxisListType.X, AluOpType.max,
+                      negate=True).then_inc(sem.s_m0, 1)
+    dve.wait_ge(sem.s_st1, NS)
+    dve.tensor_reduce(T.ngm[:, 1:2], st[1][:, 0:NS * 128], AxisListType.X, AluOpType.max,
+                      negate=True).then_inc(sem.s_m1, 1)
+    act.wait_ge(sem.s_id, 1)
+    act.wait_ge(sem.s_m0, 1)
+    act.activation(T.dg[:, 0:128], T.idn[:], Copy, scale=T.ngm[:, 0:1]).then_inc(sem.s_dg, 1)
+    dve.wait_ge(sem.s_id, 1)
+    dve.wait_ge(sem.s_m1, 1)
+    dve.tensor_scalar(T.dg[:, 128:256], T.idn[:], T.ngm[:, 1:2], None, mult).then_inc(sem.s_dg, 1)
+
+    pe.wait_ge(sem.s_c, 1)
+    pe.wait_ge(sem.s_dg, 2)
+    for p in order:
+        i = p["slot"]
+        pe.matmul(sc[i][:, 0:256], T.one[:], T.dg[:], False, True).then_inc(sem["s_S%d" % i], 1)
+        act.wait_ge(sem["s_S%d" % i], 2)
+        act.activation(T.pp[:, i * 256:(i + 1) * 256], sc[i][:, 0:256], Exp).then_inc(sem["s_P%d" % i], 1)
+
+    pe.wait_ge(sem.s_pad, 1)
+    for n, p in enumerate(order):
+        i = p["slot"]
+        pe.wait_ge(sem["s_P%d" % i], 1)
+        if vw[i]:
+            pe.wait_ge(sem["arrV%d" % i], vw[i])
+        V1 = T.kv[:, i * SW + 128:i * SW + 257]
+        for b in range(2):
+            pe.matmul(ob[b][:, 0:129], T.pp[:, i * 256 + b * 128:i * 256 + (b + 1) * 128], V1,
+                      n == 0, n == NS - 1).then_inc(sem["s_O%d" % b], 1)
+
+    dve.wait_ge(sem.s_O0, NS)
+    dve.reciprocal(T.rl[:, 0:1], ob[0][:, 128:129]).then_inc(sem.s_r0, 1)
+    dve.wait_ge(sem.s_O1, NS)
+    dve.reciprocal(T.rl[:, 1:2], ob[1][:, 128:129]).then_inc(sem.s_r1, 1)
+    dve.wait_ge(sem.s_r0, 1)
+    dve.tensor_scalar(T.ys[:, 0:128], ob[0][:, 0:128], T.rl[:, 0:1], None, mult).then_inc(sem.s_y0, 1)
+    act.wait_ge(sem.s_r1, 1)
+    act.activation(T.ys[:, 128:256], ob[1][:, 0:128], Copy, scale=T.rl[:, 1:2]).then_inc(sem.s_y1, 1)
+    sy.wait_ge(sem.s_y0, 1)
+    sy.dma_start(T.y[0:128, :], T.ys[:, 0:128]).then_inc(sem.s_o0, 16)
+    act.wait_ge(sem.s_y1, 1)
+    act.dma_start(T.y[128:256, :], T.ys[:, 128:256]).then_inc(sem.s_o1, 16)
+    sy.wait_ge(sem.s_o0, 16)
+    act.wait_ge(sem.s_o1, 16)

@@ -2,10 +2,11 @@ from concourse.bass import DstId, RemoteDMATransfer
 from concourse.mybir import AluOpType, AxisListType, ActivationFunctionType
 
 NS = 3
-SW = 264
+SW = 256
 N_ON = 4
 N_RELAY = 8
 N_DIR = 8
+BS = [(b, s) for b in range(2) for s in range(NS)]
 
 SCRATCH = {
     "qs": ("sbuf", [128, 256], "bfloat16"),
@@ -14,23 +15,22 @@ SCRATCH = {
     "vd": ("dram", [128, 128], "bfloat16"),
     "one": ("sbuf", [128, 128], "bfloat16"),
     "idn": ("sbuf", [128, 128], "bfloat16"),
-    "dg": ("sbuf", [128, 256], "bfloat16"),
     "ngm": ("sbuf", [128, 2], "float32"),
+    "ls": ("sbuf", [128, 2 * NS], "float32"),
+    "lt": ("sbuf", [128, 2], "float32"),
     "rl": ("sbuf", [128, 2], "float32"),
-    "pp": ("sbuf", [128, NS * 256], "bfloat16"),
+    "pq": ("sbuf", [128, 2 * NS * 128], "bfloat16"),
+    "pt": ("sbuf", [128, 2 * NS * 128], "bfloat16"),
     "ys": ("sbuf", [128, 256], "bfloat16"),
     "st0": ("psum", [128, 512], "float32"),
     "st1": ("psum", [128, 512], "float32"),
-    "sc0": ("psum", [128, 512], "float32"),
-    "sc1": ("psum", [128, 512], "float32"),
-    "sc2": ("psum", [128, 512], "float32"),
-    "o0": ("psum", [128, 512], "float32"),
-    "o1": ("psum", [128, 512], "float32"),
 }
-SEMAPHORES = (["s_kd", "s_vd", "s_q", "s_c", "s_id", "s_pad", "s_st0", "s_st1", "s_m0", "s_m1", "s_dg",
+for _b, _s in BS:
+    SCRATCH["tp%d%d" % (_b, _s)] = ("psum", [128, 1024], "bfloat16")
+SEMAPHORES = (["s_kd", "s_vd", "s_q", "s_one", "s_id", "s_st0", "s_st1", "s_m0", "s_m1", "s_l0", "s_l1",
                "s_O0", "s_O1", "s_r0", "s_r1", "s_y0", "s_y1", "s_o0", "s_o1", "hK", "hV", "sent"]
               + ["arrK%d" % i for i in range(NS)] + ["arrV%d" % i for i in range(NS)]
-              + ["s_S%d" % i for i in range(NS)] + ["s_P%d" % i for i in range(NS)])
+              + ["s_%s%d%d" % (n, b, s) for n in "PTC" for b, s in BS])
 
 
 def bits(m):
@@ -97,15 +97,12 @@ def rank_program(g, core, T, topo):
         act.dma_start(T.kv[:, c0 + 128:c0 + 256], T.v[:]).then_inc(sem["arrV%d" % own], 16)
     sy.dma_start(T.qs[:], T.q[:]).then_inc(sem.s_q, 16)
 
-    dve.memset(T.one[:], 1.0).then_inc(sem.s_c, 1)
-    g.wait_ge(sem.s_c, 1)
-    g.affine_select(T.idn[:], T.one[:], [[-1, 128]], AluOpType.is_equal, 0.0, 0, 1).then_inc(sem.s_id, 1)
-    act.wait_ge(sem.s_c, 1)
-    act.activation(T.kv[:, 256::SW], T.one[:, 0:NS], Exp, scale=0.0).then_inc(sem.s_pad, 1)
+    act.wait_ge(sem.s_q, 16)
+    act.activation(T.one[:], T.qs[:, 0:128], Exp, scale=0.0).then_inc(sem.s_one, 1)
 
+    sent = 0
     if mine:
         p = mine[0]
-        sent = 0
         eng = bits(topo.mask(core, p["direct"][0]))
         if p["far"]:
             ek, ev = eng[0::2][:N_ON], eng[1::2][:N_ON]
@@ -120,9 +117,13 @@ def rank_program(g, core, T, topo):
         g.remote_dma_fused([xfer(topo, T.kv[:, c0:c0 + 256], T.kv[:, c0:c0 + 256], p["direct"], ed,
                                  sem["arrK%d" % own])], local_sem=sem.sent)
         sent += len(ed)
+
+    g.wait_ge(sem.s_one, 1)
+    g.affine_select(T.idn[:], T.one[:], [[-1, 128]], AluOpType.is_equal, 0.0, 0, 1).then_inc(sem.s_id, 1)
+    if sent:
         g.wait_ge(sem.sent, sent)
 
-    order = sorted(P, key=lambda p: (p["src"] != core, p["slot"]))
+    order = [p["slot"] for p in sorted(P, key=lambda p: (p["src"] != core, p["slot"]))]
     kw, vw = {}, {}
     for p in P:
         i = p["slot"]
@@ -133,60 +134,66 @@ def rank_program(g, core, T, topo):
         else:
             kw[i], vw[i] = N_RELAY, N_RELAY
     st = [T.st0, T.st1]
-    sc = [T.sc0, T.sc1, T.sc2]
-    ob = [T.o0, T.o1]
+
+    def col(b, s):
+        return (b * NS + s) * 128
 
     pe.wait_ge(sem.s_q, 16)
-    for p in order:
-        i = p["slot"]
-        K = T.kv[:, i * SW:i * SW + 128]
-        pe.wait_ge(sem["arrK%d" % i], kw[i])
-        pe.matmul(st[0][:, i * 128:(i + 1) * 128], T.qs[:, 0:128], K, True, True).then_inc(sem.s_st0, 1)
-        pe.matmul(st[1][:, i * 128:(i + 1) * 128], T.qs[:, 128:256], K, True, True).then_inc(sem.s_st1, 1)
-        pe.matmul(sc[i][:, 0:256], K, T.qs[:], True, False).then_inc(sem["s_S%d" % i], 1)
+    jobs = [(b, s) for s in order if mine and s == own for b in range(2)]
+    jobs += [(b, s) for b in range(2) for s in order if not (mine and s == own)]
+    seen = []
+    for b, s in jobs:
+        if s not in seen:
+            pe.wait_ge(sem["arrK%d" % s], kw[s])
+            seen.append(s)
+        pe.matmul(st[b][:, s * 128:(s + 1) * 128], T.qs[:, b * 128:(b + 1) * 128], T.kv[:, s * SW:s * SW + 128],
+                  True, True).then_inc(sem["s_st%d" % b], 1)
 
-    dve.wait_ge(sem.s_st0, NS)
-    dve.tensor_reduce(T.ngm[:, 0:1], st[0][:, 0:NS * 128], AxisListType.X, AluOpType.max,
-                      negate=True).then_inc(sem.s_m0, 1)
-    dve.wait_ge(sem.s_st1, NS)
-    dve.tensor_reduce(T.ngm[:, 1:2], st[1][:, 0:NS * 128], AxisListType.X, AluOpType.max,
-                      negate=True).then_inc(sem.s_m1, 1)
-    act.wait_ge(sem.s_id, 1)
-    act.wait_ge(sem.s_m0, 1)
-    act.activation(T.dg[:, 0:128], T.idn[:], Copy, scale=T.ngm[:, 0:1]).then_inc(sem.s_dg, 1)
-    dve.wait_ge(sem.s_id, 1)
-    dve.wait_ge(sem.s_m1, 1)
-    dve.tensor_scalar(T.dg[:, 128:256], T.idn[:], T.ngm[:, 1:2], None, mult).then_inc(sem.s_dg, 1)
+    for b in range(2):
+        dve.wait_ge(sem["s_st%d" % b], NS)
+        dve.tensor_reduce(T.ngm[:, b:b + 1], st[b][:, 0:NS * 128], AxisListType.X, AluOpType.max,
+                          negate=True).then_inc(sem["s_m%d" % b], 1)
 
-    pe.wait_ge(sem.s_c, 1)
-    pe.wait_ge(sem.s_dg, 2)
-    for p in order:
-        i = p["slot"]
-        pe.matmul(sc[i][:, 0:256], T.one[:], T.dg[:], False, True).then_inc(sem["s_S%d" % i], 1)
-        act.wait_ge(sem["s_S%d" % i], 2)
-        act.activation(T.pp[:, i * 256:(i + 1) * 256], sc[i][:, 0:256], Exp).then_inc(sem["s_P%d" % i], 1)
+    pe.wait_ge(sem.s_id, 1)
+    for b in range(2):
+        act.wait_ge(sem["s_m%d" % b], 1)
+        for s in order:
+            c = col(b, s)
+            act.activation(T.pq[:, c:c + 128], st[b][:, s * 128:(s + 1) * 128], Exp, bias=T.ngm[:, b:b + 1],
+                           accum_out=T.ls[:, b * NS + s:b * NS + s + 1]).then_inc(sem["s_P%d%d" % (b, s)], 1)
+            pe.wait_ge(sem["s_P%d%d" % (b, s)], 1)
+            pe.transpose(T["tp%d%d" % (b, s)][:, 0:128], T.pq[:, c:c + 128],
+                         T.idn[:]).then_inc(sem["s_T%d%d" % (b, s)], 1)
 
-    pe.wait_ge(sem.s_pad, 1)
-    for n, p in enumerate(order):
-        i = p["slot"]
-        pe.wait_ge(sem["s_P%d" % i], 1)
-        if vw[i]:
-            pe.wait_ge(sem["arrV%d" % i], vw[i])
-        V1 = T.kv[:, i * SW + 128:i * SW + 257]
-        for b in range(2):
-            pe.matmul(ob[b][:, 0:129], T.pp[:, i * 256 + b * 128:i * 256 + (b + 1) * 128], V1,
+    for b in range(2):
+        for s in order:
+            c = col(b, s)
+            dve.wait_ge(sem["s_P%d%d" % (b, s)], 1)
+            dve.wait_ge(sem["s_T%d%d" % (b, s)], 1)
+            dve.tensor_copy(T.pt[:, c:c + 128], T["tp%d%d" % (b, s)][:, 0:128]).then_inc(sem["s_C%d%d" % (b, s)], 1)
+        dve.tensor_reduce(T.lt[:, b:b + 1], T.ls[:, b * NS:(b + 1) * NS], AxisListType.X,
+                          AluOpType.add).then_inc(sem["s_l%d" % b], 1)
+        dve.wait_ge(sem["s_l%d" % b], 1)
+        dve.reciprocal(T.rl[:, b:b + 1], T.lt[:, b:b + 1]).then_inc(sem["s_r%d" % b], 1)
+
+    for b in range(2):
+        pe.wait_ge(sem["s_m%d" % b], 1)
+        for n, s in enumerate(order):
+            c = col(b, s)
+            pe.wait_ge(sem["s_C%d%d" % (b, s)], 1)
+            if vw[s] and b == 0:
+                pe.wait_ge(sem["arrV%d" % s], vw[s])
+            pe.matmul(st[b][:, 0:128], T.pt[:, c:c + 128], T.kv[:, s * SW + 128:s * SW + 256],
                       n == 0, n == NS - 1).then_inc(sem["s_O%d" % b], 1)
 
     dve.wait_ge(sem.s_O0, NS)
-    dve.reciprocal(T.rl[:, 0:1], ob[0][:, 128:129]).then_inc(sem.s_r0, 1)
-    dve.wait_ge(sem.s_O1, NS)
-    dve.reciprocal(T.rl[:, 1:2], ob[1][:, 128:129]).then_inc(sem.s_r1, 1)
     dve.wait_ge(sem.s_r0, 1)
-    dve.tensor_scalar(T.ys[:, 0:128], ob[0][:, 0:128], T.rl[:, 0:1], None, mult).then_inc(sem.s_y0, 1)
-    act.wait_ge(sem.s_r1, 1)
-    act.activation(T.ys[:, 128:256], ob[1][:, 0:128], Copy, scale=T.rl[:, 1:2]).then_inc(sem.s_y1, 1)
+    dve.tensor_scalar(T.ys[:, 0:128], st[0][:, 0:128], T.rl[:, 0:1], None, mult).then_inc(sem.s_y0, 1)
     sy.wait_ge(sem.s_y0, 1)
     sy.dma_start(T.y[0:128, :], T.ys[:, 0:128]).then_inc(sem.s_o0, 16)
+    act.wait_ge(sem.s_O1, NS)
+    act.wait_ge(sem.s_r1, 1)
+    act.activation(T.ys[:, 128:256], st[1][:, 0:128], Copy, scale=T.rl[:, 1:2]).then_inc(sem.s_y1, 1)
     act.wait_ge(sem.s_y1, 1)
     act.dma_start(T.y[128:256, :], T.ys[:, 128:256]).then_inc(sem.s_o1, 16)
     sy.wait_ge(sem.s_o0, 16)

@@ -3,9 +3,9 @@ from concourse.mybir import AluOpType, AxisListType, ActivationFunctionType
 
 NS = 3
 SW = 256
-N_ON = 4
-N_RELAY = 8
-N_DIR = 8
+N_ON = 2
+N_SELF = 2
+N_OFF = 8
 BS = [(b, s) for b in range(2) for s in range(NS)]
 
 SCRATCH = {
@@ -13,7 +13,7 @@ SCRATCH = {
     "kv": ("sbuf", [128, NS * SW], "bfloat16"),
     "kd": ("dram", [128, 128], "bfloat16"),
     "vd": ("dram", [128, 128], "bfloat16"),
-    "one": ("sbuf", [128, 128], "bfloat16"),
+    "mm": ("sbuf", [128, 128], "bfloat16"),
     "idn": ("sbuf", [128, 128], "bfloat16"),
     "ngm": ("sbuf", [128, 2], "float32"),
     "ls": ("sbuf", [128, 2 * NS], "float32"),
@@ -27,9 +27,9 @@ SCRATCH = {
 }
 for _b, _s in BS:
     SCRATCH["tp%d%d" % (_b, _s)] = ("psum", [128, 1024], "bfloat16")
-SEMAPHORES = (["s_kd", "s_vd", "s_q", "s_one", "s_id", "s_st0", "s_st1", "s_m0", "s_m1", "s_l0", "s_l1",
+SEMAPHORES = (["s_kd", "s_vd", "s_q", "s_z", "s_c", "arrM", "s_id", "s_st0", "s_st1", "s_m0", "s_m1", "s_l0", "s_l1",
                "s_O0", "s_O1", "s_r0", "s_r1", "s_y0", "s_y1", "s_o0", "s_o1", "hK", "hV", "sent"]
-              + ["arrK%d" % i for i in range(NS)] + ["arrV%d" % i for i in range(NS)]
+              + ["%s%d" % (n, i) for n in ("arrK", "arrV", "ldK", "ldV") for i in range(NS)]
               + ["s_%s%d%d" % (n, b, s) for n in "PTC" for b, s in BS])
 
 
@@ -52,99 +52,102 @@ def xfer(topo, src_ap, dst_ap, dsts, engines, sem):
 
 def plan(T, topo):
     cores = list(T.cores)
+    srcs = [cores[j] for j in T.tables["MEM"]]
+    rest = [c for c in cores if c not in srcs]
     out = []
-    for slot, j in enumerate(T.tables["MEM"]):
-        s = cores[j]
+    for slot, s in enumerate(srcs):
         dests = [d for d in cores if d != s]
-        direct = [d for d in dests if topo.may_write(s, d)]
         far = [d for d in dests if not topo.may_write(s, d)]
+        near = [d for d in dests if topo.may_write(s, d)]
+        self_d, relay_d = near[:N_SELF], far + near[N_SELF:]
         free = [c for c in range(topo.CHIPS * topo.CORES_PER_CHIP)
                 if topo.chip(c) == topo.chip(s) and c not in cores]
-        able = [c for c in free if all(topo.may_write(c, d) for d in far)]
-        out.append({"slot": slot, "src": s, "direct": direct, "far": far,
-                    "kh": [c for c in able if topo.die(c) == topo.die(s)][0],
-                    "vh": [c for c in able if topo.die(c) != topo.die(s)][0]})
+        pool = [c for c in free if topo.die(c) == topo.die(s)]
+        kh = []
+        for d in relay_d:
+            c = [c for c in pool if topo.may_write(c, d)][0]
+            pool.remove(c)
+            kh.append((c, [d]))
+        vh = [c for c in free if topo.die(c) != topo.die(s) and all(topo.may_write(c, d) for d in dests)][0]
+        cut = {kh[0][0]: (rest[slot], 0), vh: (rest[slot], 1), kh[1][0]: (s, 0), kh[2][0]: (s, 1)}
+        out.append({"slot": slot, "src": s, "self": self_d, "kh": kh, "vh": (vh, relay_d), "cut": cut})
     return out
 
 
 def rank_program(g, core, T, topo):
     sem = T.sem
     P = plan(T, topo)
+    pe, dve, act, sy = g.tensor, g.vector, g.scalar, g.sync
 
     for p in P:
-        c0 = p["slot"] * SW
-        for who, hs, buf, off, arr in (("kh", sem.hK, T.kd, 0, "arrK%d"), ("vh", sem.hV, T.vd, 128, "arrV%d")):
-            if p["far"] and core == p[who]:
-                e = pick(bits(topo.mask(core, p["far"][0])), N_RELAY)
-                g.wait_ge(hs, N_ON)
-                g.remote_dma_fused([xfer(topo, buf[:], T.kv[:, c0 + off:c0 + off + 128], p["far"], e,
-                                         sem[arr % p["slot"]])], local_sem=sem.sent)
-                g.wait_ge(sem.sent, len(e))
-                return
+        i = p["slot"]
+        c0 = i * SW
+        work = [(c, d, sem.hK, T.kd, c0, "arrK%d" % i) for c, d in p["kh"]]
+        work.append((p["vh"][0], p["vh"][1], sem.hV, T.vd, c0 + 128, "arrV%d" % i))
+        for c, dsts, hs, buf, off, arr in work:
+            if core != c:
+                continue
+            e = pick(bits(topo.mask(core, dsts[0])), N_OFF)
+            who, h = p["cut"][core]
+            half = T.mm[:, h * 64:(h + 1) * 64]
+            dve.memset(half, 0.0).then_inc(sem.s_z, 1)
+            g.wait_ge(sem.s_z, 1)
+            g.affine_select(half, half, [[-1, 64]], AluOpType.is_equal, -200.0, -64 * h, 1).then_inc(sem.s_c, 1)
+            g.wait_ge(sem.s_c, 1)
+            g.remote_dma_fused([xfer(topo, half, half, [who], e, sem.arrM)], local_sem=sem.sent)
+            g.wait_ge(hs, N_ON)
+            g.remote_dma_fused([xfer(topo, buf[:], T.kv[:, off:off + 128], dsts, e, sem[arr])], local_sem=sem.sent)
+            g.wait_ge(sem.sent, 2 * len(e))
+            return
     if T.rank_of(core) is None:
         return
 
     mine = [p for p in P if p["src"] == core]
-    pe, dve, act, sy = g.tensor, g.vector, g.scalar, g.sync
+    own = mine[0]["slot"] if mine else None
     mult, Exp, Copy = AluOpType.mult, ActivationFunctionType.Exp, ActivationFunctionType.Copy
 
     if mine:
-        c0 = mine[0]["slot"] * SW
-        own = mine[0]["slot"]
+        c0 = own * SW
         sy.dma_start(T.kd[:], T.k[:]).then_inc(sem.s_kd, 16)
         act.dma_start(T.vd[:], T.v[:]).then_inc(sem.s_vd, 16)
-        sy.dma_start(T.kv[:, c0:c0 + 128], T.k[:]).then_inc(sem["arrK%d" % own], 16)
-        act.dma_start(T.kv[:, c0 + 128:c0 + 256], T.v[:]).then_inc(sem["arrV%d" % own], 16)
+        sy.dma_start(T.kv[:, c0:c0 + 128], T.k[:]).then_inc(sem["ldK%d" % own], 16)
+        act.dma_start(T.kv[:, c0 + 128:c0 + 256], T.v[:]).then_inc(sem["ldV%d" % own], 16)
     sy.dma_start(T.qs[:], T.q[:]).then_inc(sem.s_q, 16)
 
-    act.wait_ge(sem.s_q, 16)
-    act.activation(T.one[:], T.qs[:, 0:128], Exp, scale=0.0).then_inc(sem.s_one, 1)
-
-    sent = 0
     if mine:
         p = mine[0]
-        eng = bits(topo.mask(core, p["direct"][0]))
-        if p["far"]:
-            ek, ev = eng[0::2][:N_ON], eng[1::2][:N_ON]
-            g.wait_ge(sem.s_kd, 16)
-            g.wait_ge(sem.s_vd, 16)
-            g.remote_dma_fused([xfer(topo, T.kd[:], T.kd[:], [p["kh"]], ek, sem.hK),
-                                xfer(topo, T.vd[:], T.vd[:], [p["vh"]], ev, sem.hV)], local_sem=sem.sent)
-            sent += len(ek) + len(ev)
-        ed = pick(eng, N_DIR)
-        g.wait_ge(sem["arrK%d" % own], 16)
-        g.wait_ge(sem["arrV%d" % own], 16)
-        g.remote_dma_fused([xfer(topo, T.kv[:, c0:c0 + 256], T.kv[:, c0:c0 + 256], p["direct"], ed,
-                                 sem["arrK%d" % own])], local_sem=sem.sent)
-        sent += len(ed)
+        eng = pick(bits(topo.mask(core, p["self"][0])), N_OFF)
+        ev = eng[0:2 * N_ON:2]
+        ek = [e for e in eng if e not in ev]
+        g.wait_ge(sem.s_kd, 16)
+        g.wait_ge(sem.s_vd, 16)
+        g.remote_dma_fused([xfer(topo, T.kd[:], T.kd[:], [c], ek[n * N_ON:(n + 1) * N_ON], sem.hK)
+                            for n, (c, d) in enumerate(p["kh"])]
+                           + [xfer(topo, T.vd[:], T.vd[:], [p["vh"][0]], ev, sem.hV)], local_sem=sem.sent)
+        g.remote_dma_fused([xfer(topo, T.kd[:], T.kv[:, c0:c0 + 128], p["self"], eng, sem["arrK%d" % own])],
+                           local_sem=sem.sent)
+        g.remote_dma_fused([xfer(topo, T.vd[:], T.kv[:, c0 + 128:c0 + 256], p["self"], eng, sem["arrV%d" % own])],
+                           local_sem=sem.sent)
+        g.wait_ge(sem.sent, 3 * len(eng))
 
-    g.wait_ge(sem.s_one, 1)
-    g.affine_select(T.idn[:], T.one[:], [[-1, 128]], AluOpType.is_equal, 0.0, 0, 1).then_inc(sem.s_id, 1)
-    if sent:
-        g.wait_ge(sem.sent, sent)
+    act.wait_ge(sem.arrM, 2 * N_OFF)
+    act.activation(T.idn[:], T.mm[:], Exp).then_inc(sem.s_id, 1)
 
     order = [p["slot"] for p in sorted(P, key=lambda p: (p["src"] != core, p["slot"]))]
-    kw, vw = {}, {}
-    for p in P:
-        i = p["slot"]
-        if p["src"] == core:
-            kw[i], vw[i] = 16, 16
-        elif core in p["direct"]:
-            kw[i], vw[i] = N_DIR, 0
-        else:
-            kw[i], vw[i] = N_RELAY, N_RELAY
+    kw = {s: ("ldK%d" % s, 16) if s == own else ("arrK%d" % s, N_OFF) for s in order}
+    vw = {s: ("ldV%d" % s, 16) if s == own else ("arrV%d" % s, N_OFF) for s in order}
     st = [T.st0, T.st1]
 
     def col(b, s):
         return (b * NS + s) * 128
 
     pe.wait_ge(sem.s_q, 16)
-    jobs = [(b, s) for s in order if mine and s == own for b in range(2)]
-    jobs += [(b, s) for b in range(2) for s in order if not (mine and s == own)]
+    jobs = [(b, s) for s in order if s == own for b in range(2)]
+    jobs += [(b, s) for b in range(2) for s in order if s != own]
     seen = []
     for b, s in jobs:
         if s not in seen:
-            pe.wait_ge(sem["arrK%d" % s], kw[s])
+            pe.wait_ge(sem[kw[s][0]], kw[s][1])
             seen.append(s)
         pe.matmul(st[b][:, s * 128:(s + 1) * 128], T.qs[:, b * 128:(b + 1) * 128], T.kv[:, s * SW:s * SW + 128],
                   True, True).then_inc(sem["s_st%d" % b], 1)
@@ -181,8 +184,8 @@ def rank_program(g, core, T, topo):
         for n, s in enumerate(order):
             c = col(b, s)
             pe.wait_ge(sem["s_C%d%d" % (b, s)], 1)
-            if vw[s] and b == 0:
-                pe.wait_ge(sem["arrV%d" % s], vw[s])
+            if b == 0:
+                pe.wait_ge(sem[vw[s][0]], vw[s][1])
             pe.matmul(st[b][:, 0:128], T.pt[:, c:c + 128], T.kv[:, s * SW + 128:s * SW + 256],
                       n == 0, n == NS - 1).then_inc(sem["s_O%d" % b], 1)
 

from concourse.bass import DstId, RemoteDMATransfer
from concourse.mybir import AluOpType, AxisListType, ActivationFunctionType

NS = 3
SW = 256
N_ON = 2
N_SELF = 2
N_OFF = 8
BS = [(b, s) for b in range(2) for s in range(NS)]

SCRATCH = {
    "qs": ("sbuf", [128, 256], "bfloat16"),
    "kv": ("sbuf", [128, NS * SW], "bfloat16"),
    "kd": ("dram", [128, 128], "bfloat16"),
    "vd": ("dram", [128, 128], "bfloat16"),
    "mm": ("sbuf", [128, 128], "bfloat16"),
    "idn": ("sbuf", [128, 128], "bfloat16"),
    "ngm": ("sbuf", [128, 2], "float32"),
    "ls": ("sbuf", [128, 2 * NS], "float32"),
    "lt": ("sbuf", [128, 2], "float32"),
    "rl": ("sbuf", [128, 2], "float32"),
    "pq": ("sbuf", [128, 2 * NS * 128], "bfloat16"),
    "pt": ("sbuf", [128, 2 * NS * 128], "bfloat16"),
    "ys": ("sbuf", [128, 256], "bfloat16"),
    "st0": ("psum", [128, 512], "float32"),
    "st1": ("psum", [128, 512], "float32"),
}
for _b, _s in BS:
    SCRATCH["tp%d%d" % (_b, _s)] = ("psum", [128, 1024], "bfloat16")
SEMAPHORES = (["s_kd", "s_vd", "s_q", "s_z", "s_c", "arrM", "s_id", "s_st0", "s_st1", "s_m0", "s_m1", "s_l0", "s_l1",
               "s_O0", "s_O1", "s_r0", "s_r1", "s_y0", "s_y1", "s_o0", "s_o1", "hK", "hV", "sent"]
              + ["%s%d" % (n, i) for n in ("arrK", "arrV", "ldK", "ldV") for i in range(NS)]
              + ["s_%s%d%d" % (n, b, s) for n in "PTC" for b, s in BS])


def bits(m):
    return [e for e in range(m.bit_length()) if (m >> e) & 1]


def pick(es, n):
    return es[::len(es) // n][:n]


def xfer(topo, src_ap, dst_ap, dsts, engines, sem):
    ids = []
    for d in dsts:
        a = topo.addr(d)
        ids.append(DstId(rid=a[0], pnc=a[1]))
    return RemoteDMATransfer(dst_ids=ids, dma_engine_mask=sum(1 << e for e in engines), remote_sem=sem,
                             srcs=[src_ap], dsts=[dst_ap] * len(dsts), alu_op=0)


def plan(T, topo):
    cores = list(T.cores)
    srcs = [cores[j] for j in T.tables["MEM"]]
    rest = [c for c in cores if c not in srcs]
    out = []
    for slot, s in enumerate(srcs):
        dests = [d for d in cores if d != s]
        far = [d for d in dests if not topo.may_write(s, d)]
        near = [d for d in dests if topo.may_write(s, d)]
        self_d, relay_d = near[:N_SELF], far + near[N_SELF:]
        free = [c for c in range(topo.CHIPS * topo.CORES_PER_CHIP)
                if topo.chip(c) == topo.chip(s) and c not in cores]
        pool = [c for c in free if topo.die(c) == topo.die(s)]
        kh = []
        for d in relay_d:
            c = [c for c in pool if topo.may_write(c, d)][0]
            pool.remove(c)
            kh.append((c, [d]))
        vh = [c for c in free if topo.die(c) != topo.die(s) and all(topo.may_write(c, d) for d in dests)][0]
        cut = {kh[0][0]: (rest[slot], 0), vh: (rest[slot], 1), kh[1][0]: (s, 0), kh[2][0]: (s, 1)}
        out.append({"slot": slot, "src": s, "self": self_d, "kh": kh, "vh": (vh, relay_d), "cut": cut})
    return out


def rank_program(g, core, T, topo):
    sem = T.sem
    P = plan(T, topo)
    pe, dve, act, sy = g.tensor, g.vector, g.scalar, g.sync

    for p in P:
        i = p["slot"]
        c0 = i * SW
        work = [(c, d, sem.hK, T.kd, c0, "arrK%d" % i) for c, d in p["kh"]]
        work.append((p["vh"][0], p["vh"][1], sem.hV, T.vd, c0 + 128, "arrV%d" % i))
        for c, dsts, hs, buf, off, arr in work:
            if core != c:
                continue
            e = pick(bits(topo.mask(core, dsts[0])), N_OFF)
            who, h = p["cut"][core]
            half = T.mm[:, h * 64:(h + 1) * 64]
            dve.memset(half, 0.0).then_inc(sem.s_z, 1)
            g.wait_ge(sem.s_z, 1)
            g.affine_select(half, half, [[-1, 64]], AluOpType.is_equal, -200.0, -64 * h, 1).then_inc(sem.s_c, 1)
            g.wait_ge(sem.s_c, 1)
            g.remote_dma_fused([xfer(topo, half, half, [who], e, sem.arrM)], local_sem=sem.sent)
            g.wait_ge(hs, N_ON)
            g.remote_dma_fused([xfer(topo, buf[:], T.kv[:, off:off + 128], dsts, e, sem[arr])], local_sem=sem.sent)
            g.wait_ge(sem.sent, 2 * len(e))
            return
    if T.rank_of(core) is None:
        return

    mine = [p for p in P if p["src"] == core]
    own = mine[0]["slot"] if mine else None
    mult, Exp, Copy = AluOpType.mult, ActivationFunctionType.Exp, ActivationFunctionType.Copy

    if mine:
        c0 = own * SW
        sy.dma_start(T.kd[:], T.k[:]).then_inc(sem.s_kd, 16)
        act.dma_start(T.vd[:], T.v[:]).then_inc(sem.s_vd, 16)
        sy.dma_start(T.kv[:, c0:c0 + 128], T.k[:]).then_inc(sem["ldK%d" % own], 16)
        act.dma_start(T.kv[:, c0 + 128:c0 + 256], T.v[:]).then_inc(sem["ldV%d" % own], 16)
    sy.dma_start(T.qs[:], T.q[:]).then_inc(sem.s_q, 16)

    if mine:
        p = mine[0]
        eng = pick(bits(topo.mask(core, p["self"][0])), N_OFF)
        ev = eng[0:2 * N_ON:2]
        ek = [e for e in eng if e not in ev]
        g.wait_ge(sem.s_kd, 16)
        g.wait_ge(sem.s_vd, 16)
        g.remote_dma_fused([xfer(topo, T.kd[:], T.kd[:], [c], ek[n * N_ON:(n + 1) * N_ON], sem.hK)
                            for n, (c, d) in enumerate(p["kh"])]
                           + [xfer(topo, T.vd[:], T.vd[:], [p["vh"][0]], ev, sem.hV)], local_sem=sem.sent)
        g.remote_dma_fused([xfer(topo, T.kd[:], T.kv[:, c0:c0 + 128], p["self"], eng, sem["arrK%d" % own])],
                           local_sem=sem.sent)
        g.remote_dma_fused([xfer(topo, T.vd[:], T.kv[:, c0 + 128:c0 + 256], p["self"], eng, sem["arrV%d" % own])],
                           local_sem=sem.sent)
        g.wait_ge(sem.sent, 3 * len(eng))

    act.wait_ge(sem.arrM, 2 * N_OFF)
    act.activation(T.idn[:], T.mm[:], Exp).then_inc(sem.s_id, 1)

    order = [p["slot"] for p in sorted(P, key=lambda p: (p["src"] != core, p["slot"]))]
    kw = {s: ("ldK%d" % s, 16) if s == own else ("arrK%d" % s, N_OFF) for s in order}
    vw = {s: ("ldV%d" % s, 16) if s == own else ("arrV%d" % s, N_OFF) for s in order}
    st = [T.st0, T.st1]

    def col(b, s):
        return (b * NS + s) * 128

    pe.wait_ge(sem.s_q, 16)
    jobs = [(b, s) for s in order if s == own for b in range(2)]
    jobs += [(b, s) for b in range(2) for s in order if s != own]
    seen = []
    for b, s in jobs:
        if s not in seen:
            pe.wait_ge(sem[kw[s][0]], kw[s][1])
            seen.append(s)
        pe.matmul(st[b][:, s * 128:(s + 1) * 128], T.qs[:, b * 128:(b + 1) * 128], T.kv[:, s * SW:s * SW + 128],
                  True, True).then_inc(sem["s_st%d" % b], 1)

    for b in range(2):
        dve.wait_ge(sem["s_st%d" % b], NS)
        dve.tensor_reduce(T.ngm[:, b:b + 1], st[b][:, 0:NS * 128], AxisListType.X, AluOpType.max,
                          negate=True).then_inc(sem["s_m%d" % b], 1)

    pe.wait_ge(sem.s_id, 1)
    for b in range(2):
        act.wait_ge(sem["s_m%d" % b], 1)
        for s in order:
            c = col(b, s)
            act.activation(T.pq[:, c:c + 128], st[b][:, s * 128:(s + 1) * 128], Exp, bias=T.ngm[:, b:b + 1],
                           accum_out=T.ls[:, b * NS + s:b * NS + s + 1]).then_inc(sem["s_P%d%d" % (b, s)], 1)
            pe.wait_ge(sem["s_P%d%d" % (b, s)], 1)
            pe.transpose(T["tp%d%d" % (b, s)][:, 0:128], T.pq[:, c:c + 128],
                         T.idn[:]).then_inc(sem["s_T%d%d" % (b, s)], 1)

    for b in range(2):
        for s in order:
            c = col(b, s)
            dve.wait_ge(sem["s_P%d%d" % (b, s)], 1)
            dve.wait_ge(sem["s_T%d%d" % (b, s)], 1)
            dve.tensor_copy(T.pt[:, c:c + 128], T["tp%d%d" % (b, s)][:, 0:128]).then_inc(sem["s_C%d%d" % (b, s)], 1)
        dve.tensor_reduce(T.lt[:, b:b + 1], T.ls[:, b * NS:(b + 1) * NS], AxisListType.X,
                          AluOpType.add).then_inc(sem["s_l%d" % b], 1)
        dve.wait_ge(sem["s_l%d" % b], 1)
        dve.reciprocal(T.rl[:, b:b + 1], T.lt[:, b:b + 1]).then_inc(sem["s_r%d" % b], 1)

    for b in range(2):
        pe.wait_ge(sem["s_m%d" % b], 1)
        for n, s in enumerate(order):
            c = col(b, s)
            pe.wait_ge(sem["s_C%d%d" % (b, s)], 1)
            if b == 0:
                pe.wait_ge(sem[vw[s][0]], vw[s][1])
            pe.matmul(st[b][:, 0:128], T.pt[:, c:c + 128], T.kv[:, s * SW + 128:s * SW + 256],
                      n == 0, n == NS - 1).then_inc(sem["s_O%d" % b], 1)

    dve.wait_ge(sem.s_O0, NS)
    dve.wait_ge(sem.s_r0, 1)
    dve.tensor_scalar(T.ys[:, 0:128], st[0][:, 0:128], T.rl[:, 0:1], None, mult).then_inc(sem.s_y0, 1)
    sy.wait_ge(sem.s_y0, 1)
    sy.dma_start(T.y[0:128, :], T.ys[:, 0:128]).then_inc(sem.s_o0, 16)
    act.wait_ge(sem.s_O1, NS)
    act.wait_ge(sem.s_r1, 1)
    act.activation(T.ys[:, 128:256], st[1][:, 0:128], Copy, scale=T.rl[:, 1:2]).then_inc(sem.s_y1, 1)
    act.wait_ge(sem.s_y1, 1)
    act.dma_start(T.y[128:256, :], T.ys[:, 128:256]).then_inc(sem.s_o1, 16)
    sy.wait_ge(sem.s_o0, 16)
    act.wait_ge(sem.s_o1, 16)
